import numpy as np, ml_dtypes
CORES = [66,74,82,90,194,202,210,218]
N = 8
BF = ml_dtypes.bfloat16
def gentries(a):
    return np.ascontiguousarray(a.reshape(8, 16, -1).transpose(0, 2, 1)).reshape(8, -1)
def gtable(e):
    e = np.asarray(e); return np.ascontiguousarray(e.reshape(8, -1, 16).transpose(0, 2, 1)).reshape(128, -1).astype(np.int32)
D, UG, B, A, NB, KG = 3, 8, 6, 2, 32, 16
U, V, E, S, K = 8 * UG, 2 ** B, 2 ** (A * B), 16 * NB, 8 * KG // N
def stored(c):
    return np.ascontiguousarray(c.reshape(N, 8, UG, NB, 16).transpose(0, 1, 4, 3, 2)).reshape(N, 128, -1).astype(np.int32)
def unstored(x):
    return np.ascontiguousarray(x.reshape(N, 8, 16, NB, UG).transpose(0, 1, 4, 3, 2)).reshape(N, U, S).astype(np.int64)
def pack(t, c, gv, wr):
    return {"tb": t.reshape(N, 8, -1).astype(np.float32).astype(BF), "x": stored(c), "give": np.stack([gtable(v.reshape(8, -1)) for v in gv]), "wires": np.stack([gtable(v.reshape(8, -1)) for v in wr])}
def draw(rng):
    return rng.integers(0, V, (N, 8, D, UG, E)), rng.integers(0, V, (N, U, S)), rng.integers(0, U, (N, 8, D, KG)), rng.integers(0, N * K, (N, 8, D, A, UG))
def setup_inputs(rng):
    return pack(*draw(rng))
def setup_inputs_ends(rng):
    t, c, gv, wr = draw(rng)
    t = rng.integers(0, 2, t.shape) * (V - 1); t[..., 0] = 0; t[..., E - 1] = V - 1; c = rng.integers(0, 2, c.shape) * (V - 1); c[:, :, 0] = 0; c[:, :, S - 1] = V - 1
    gv = rng.choice(np.array([0, UG - 1, UG, 7 * UG, U - 1]), gv.shape); wr = rng.choice(np.array([0, K - 1, K, N * K - K, N * K - 1]), wr.shape)
    return pack(t, c, gv, wr)
def setup_inputs_one(rng):
    t, c, gv, wr = draw(rng)
    gv[:] = gv[..., :1].copy(); wr[:] = wr[:, :, :, :1].copy(); q = rng.integers(0, N); wr[q] = wr[q][..., :1].copy()
    return pack(t, c, gv, wr)
def setup_inputs_next(rng):
    t, c, gv, wr = draw(rng)
    i = rng.integers(0, 2, (N, 8, D, UG, 1)) * (A - 1); t = (np.arange(E) >> (B * (A - 1 - i))) & (V - 1)
    wr = wr % K + K * ((np.arange(N) + 1) % N).reshape(N, 1, 1, 1, 1)
    return pack(t, c, gv, wr)
def setup_inputs_spread(rng):
    t, c, gv, wr = draw(rng)
    t = t >> rng.integers(0, B + 1, (N, 8, D, UG, 1)); c = c >> rng.integers(0, B + 1, (N, U, 1))
    gv = (rng.random(gv.shape) ** 3 * U).astype(np.int64); wr = (rng.random(wr.shape) ** 3 * (N * K)).astype(np.int64)
    return pack(t, c, gv, wr)
def check_inputs(d):
    bad = []
    for name, top in (("x", V), ("give", U), ("wires", N * K)):
        if not ((d[name] >= 0) & (d[name] < top)).all(): bad.append(name)
    t = d["tb"].astype(np.float32)
    if not ((t >= 0) & (t < V) & (np.floor(t) == t)).all(): bad.append("tb")
    return bad
def reference(tb, x, give, wires):
    t = tb.astype(np.float32).astype(np.int64).reshape(N, 8, D, UG, E)
    gv = np.stack([gentries(v) for v in give]).reshape(N, 8 * D * KG).reshape(N, 8, D, KG)
    wr = np.stack([gentries(v) for v in wires]).reshape(N, 8, D, A, UG)
    c = unstored(x)
    for l in range(D):
        lines = np.zeros((N, N * K, S), np.int64); new = np.zeros((N, U, S), np.int64)
        for q in range(N):
            lines[:, q * K:(q + 1) * K] = c[q][gv[q, :, l].reshape(-1)].reshape(N, K, S)
        for r in range(N):
            a = np.zeros((8, UG, S), np.int64)
            for i in range(A):
                a = a * V + lines[r][wr[r, :, l, i]]
            new[r] = np.take_along_axis(t[r, :, l], a, axis=2).reshape(U, S)
        c = new
    return {"y": np.asarray(stored(c), np.float32)}

@@ -1,0 +1,220 @@
+from concourse.bass import DstId, RemoteDMATransfer
+from concourse.mybir import AluOpType, ActivationFunctionType
+
+L = 3
+SCRATCH = {"xt": ("sbuf", [128, 8, 2, 16], "bfloat16"), "xu": ("sbuf", [128, 2, 128], "bfloat16"),
+           "dsf": ("sbuf", [128, 8, 4, 8], "bfloat16"), "lists": ("sbuf", [128, 192], "uint16")}
+for _n, _w in (("xi", 256), ("gw", 6), ("pidx", 2), ("pint", 2)):
+    SCRATCH[_n] = ("sbuf", [128, _w], "int32")
+for _n, _w in (("gwf", 6), ("pf", 2), ("ki", 128), ("cg", 32), ("cw", 32), ("xzi", 320), ("zi", 288), ("pii", 128),
+               ("sli", 64), ("slj", 64), ("yt", 256)):
+    SCRATCH[_n] = ("sbuf", [128, _w], "float32")
+for _n, _w in (("xb", 256), ("rep", 128), ("xz", 320), ("z1", 288), ("z64", 288), ("zf", 288), ("pim", 128), ("sel", 64),
+               ("sel2", 64), ("rl", 192)):
+    SCRATCH[_n] = ("sbuf", [128, _w], "bfloat16")
+for _n in ("pa", "pb", "pl", "dt0", "dt1", "dt2", "dt3"):
+    SCRATCH[_n] = ("psum", [128, 512], "float32")
+SEMAPHORES = ["qg", "qv", "qs", "qp", "ldx", "ldg", "sty0", "sty1"]
+for _l in range(L):
+    for _n, _w in (("ds", [256]), ("send", [512]), ("land", [512]), ("c", [512]), ("o", [4, 1024]), ("tab", [4096])):
+        SCRATCH["%s%d" % (_n, _l)] = ("sbuf", [128] + _w, "bfloat16")
+    SCRATCH["tt%d" % _l] = ("sbuf", [128, 256], "float32")
+    SCRATCH["of%d" % _l] = ("sbuf", [128, 256], "uint16")
+    SEMAPHORES += ["arr%d" % _l, "sent%d" % _l, "tb%d" % _l]
+
+ORDER = [[0, 1, 4, 5, 2, 3, 6, 7], list(range(8)), list(range(8))]
+PAIRS = [[(0, 4), (1, 5), (2, 6), (3, 7)], [(0, 1), (2, 3), (4, 5), (6, 7)], [(0, 1), (2, 3), (4, 5), (6, 7)]]
+
+
+def rank_program(g, core, T, topo):
+    rank = T.rank_of(core)
+    if rank is None:
+        return
+    A = AluOpType
+    n = len(T.cores)
+    q = {"g": g, "v": g.vector, "s": g.scalar, "p": g.tensor, "y": g.sync}
+    cnt = {"g": 0, "v": 0, "s": 0, "p": 0}
+    seen = {}
+    V = g.vector
+
+    def done(k, instr):
+        cnt[k] += 1
+        instr.then_inc(T.sem["q" + k], 1)
+        return ("q" + k, cnt[k])
+
+    def need(k, *toks):
+        for sem, val in toks:
+            if seen.get((k, sem), 0) < val:
+                q[k].wait_ge(T.sem[sem], val)
+                seen[(k, sem)] = val
+
+    def mm(out, lhsT, rhs, start=True, stop=True):
+        return done("p", g.tensor.matmul(out, lhsT, rhs, start, stop))
+
+    def copy(k, out, in_, *toks):
+        need(k, *toks)
+        if k == "v":
+            return done("v", V.tensor_copy(out, in_))
+        return done("s", g.scalar.activation(out, in_, ActivationFunctionType.Copy))
+
+    def tables(l):
+        w = 8 * 4096
+        return T.tb[:, l * w:(l + 1) * w]
+
+    g.sync.dma_start(T.xi[:], T.x[:]).then_inc(T.sem.ldx, 16)
+    g.scalar.dma_start(T.gw[:, 0:3], T.give[:]).then_inc(T.sem.ldg, 16)
+    g.scalar.dma_start(T.gw[:, 3:6], T.wires[:]).then_inc(T.sem.ldg, 16)
+    g.sync.dma_start(T.tab0[0::2, :], tables(0)).then_inc(T.sem.tb0, 16)
+    g.scalar.dma_start(T.tab0[1::2, :], tables(0)).then_inc(T.sem.tb0, 16)
+
+    def iota(out, pattern, base, cm):
+        return done("g", g.iota(out[:], pattern, base, cm, allow_small_or_imprecise_dtypes=True))
+
+    i_p = done("g", g.iota(T.pidx[:], [[0, 2]], 0, 1))
+    i_k = iota(T.ki, [[0, 8], [1, 4], [0, 4]], 0, 0)
+    i_cg = iota(T.cg, [[1, 32]], 0, 0)
+    i_xz = iota(T.xzi, [[32, 5], [1000, 2], [1, 32]], -1000, -1)
+    i_cw = iota(T.cw, [[2, 4], [8, 4], [1, 2]], 0, 0)
+    i_z = iota(T.zi, [[16, 9], [1000, 2], [1, 16]], -1000, -1)
+    i_s = iota(T.sli, [[2, 8], [16, 8]], 0, -1)
+    i_s2 = iota(T.slj, [[2, 8], [16, 2], [32, 4]], 0, -1)
+    i_pi = iota(T.pii, [[32, 4], [1, 4], [4, 8]], 0, -1)
+
+    def zeros_of(out, in_, tok):
+        need("v", tok)
+        return done("v", V.tensor_scalar(out[:], in_[:], 0.0, None, A.is_equal))
+
+    need("v", i_p)
+    done("v", V.tensor_scalar(T.pint[:, 0:1], T.pidx[:, 0:1], 3, None, A.bitwise_and))
+    k = done("v", V.tensor_scalar(T.pint[:, 1:2], T.pidx[:, 1:2], 2, None, A.arith_shift_right))
+    k_pf = copy("v", T.pf[:], T.pint[:], k)
+    pm, pd = T.pf[:, 0:1], T.pf[:, 1:2]
+    need("v", k_pf, i_k)
+    k_rep = done("v", V.tensor_scalar(T.rep[:], T.ki[:], pm, None, A.is_equal))
+    k_xz = zeros_of(T.xz, T.xzi, i_xz)
+
+    def rlist(l, which):
+        a = 64 * l + 32 * which
+        j = 3 * which + l
+        src = T.cw if which else T.cg
+        return done("v", V.tensor_scalar(T.rl[:, a:a + 32], src[:], pd, T.gwf[:, j:j + 1], A.is_equal, A.mult))
+
+    def lists(a, b, tok):
+        need("p", k_rep, tok)
+        need("v", mm(T.pl[:, a:b], T.rep[:], T.rl[:, a:b]))
+        return done("v", V.tensor_scalar(T.lists[:, a:b], T.pl[:, a:b], 4.0, pm, A.mult, A.add))
+
+    k = copy("v", T.gwf[:], T.gw[:], ("ldg", 32))
+    need("v", k, i_cg)
+    k_r = rlist(0, 0)
+
+    for t in range(4):
+        k = copy("v", T.xb[:, t::4], T.xi[:, 64 * t:64 * t + 64], ("ldx", 16))
+    need("v", k)
+    k_xt = done("v", V.transpose(T.xt[:], T.xb[:]))
+    k_u = [copy(k, T.xu[:, j, :], T.xt[:, :, j, :], k_xt) for j, k in enumerate("vs")]
+    k_list = {0: lists(0, 32, k_r)}
+    need("p", k_xz)
+    ds_ready = []
+    for h in range(2):
+        for g2 in range(2):
+            a = (32 if g2 == 0 else 0) + 128 * h
+            need("p", k_u[g2])
+            k = mm(T["dt%d" % h][:, 0:128], T.xu[:, g2, :], T.xz[:, a:a + 128], g2 == 0, g2 == 1)
+        ds_ready.append(copy("sv"[h], T.ds0[:, 128 * h:128 * h + 128], T["dt%d" % h][:, 0:128], k))
+
+    for l in range(L):
+        ds, send, land, c = T["ds%d" % l], T["send%d" % l], T["land%d" % l], T["c%d" % l]
+        tt, of, o, tab = T["tt%d" % l], T["of%d" % l], T["o%d" % l], T["tab%d" % l]
+        arr, sent = ("arr%d" % l, n - 1), ("sent%d" % l, n - 1)
+        la = 64 * l
+        last = l == L - 1
+        k_sd = [copy(k, send[:, 256 * j:256 * j + 256], ds[:].indirect(T.lists[:, la + 16 * j:la + 16 * j + 16]),
+                     k_list[l], *ds_ready) for j, k in enumerate("vs")]
+        need("g", *k_sd)
+        tr = []
+        for j in range(n - 1):
+            r = (rank + 1 + j) % n
+            rid, pid = topo.addr(T.cores[r], core)
+            eng = topo.engines(core, T.cores[r])
+            tr.append(RemoteDMATransfer(dst_ids=[DstId(rid=rid, pnc=pid)], dma_engine_mask=1 << eng[j % len(eng)],
+                                        remote_sem=T.sem["arr%d" % l], src=send[:, 64 * r:64 * r + 64],
+                                        dst=land[:, 64 * rank:64 * rank + 64]))
+        g.remote_dma_fused(tr, local_sem=T.sem["sent%d" % l])
+        k_own = copy("v", land[:, 64 * rank:64 * rank + 64], send[:, 64 * rank:64 * rank + 64], *k_sd)
+        if not last:
+            need("y", sent)
+            for h in range(2):
+                g.sync.dma_start(T["tab%d" % (l + 1)][h::2, :], tables(l + 1)).then_inc(T.sem["tb%d" % (l + 1)], 16)
+        else:
+            need("g", sent)
+        if l == 0:
+            need("v", i_cw)
+            k_wl = {0: lists(32, 64, rlist(0, 1))}
+            k_z1 = zeros_of(T.z1, T.zi, i_z)
+            k_z64 = done("v", V.tensor_scalar(T.z64[:], T.zi[:], 0.0, 64.0, A.is_equal, A.mult))
+            k_sel = zeros_of(T.sel, T.sli, i_s)
+            for m, w in ((1, 0), (1, 1), (2, 0), (2, 1)):
+                k_r = rlist(m, w)
+            k = lists(64, 192, k_r)
+            for m in (1, 2):
+                k_list[m] = k_wl[m] = k
+        elif l == 1:
+            k_sel2 = zeros_of(T.sel2, T.slj, i_s2)
+            need("p", zeros_of(T.pim, T.pii, i_pi))
+            k_zf = copy("s", T.zf[:], T.pl[:, 192:480], mm(T.pl[:, 192:480], T.pim[:], T.z1[:]))
+        k_c = [copy(k, c[:, 256 * j:256 * j + 256], land[:].indirect(T.lists[:, la + 32 + 16 * j:la + 48 + 16 * j]),
+                    arr, k_wl[l], k_own) for j, k in enumerate("vs")]
+        need("p", k_z1, k_z64)
+        order = ORDER[l]
+        w = 2 if l == 0 else 4
+        half = []
+        for h, bank in enumerate((T.pa, T.pb)):
+            for b in range(0, 4, w):
+                for j in range(4):
+                    g2, i = j // 2, j % 2
+                    need("p", k_c[g2])
+                    a = (16 if g2 == 0 else 0) + 32 * order[4 * h + b]
+                    z = T.z1 if i else T.z64
+                    k = mm(bank[:, 32 * b:32 * (b + w)], c[:, 128 * j:128 * j + 128], z[:, a:a + 32 * w], j == 0, j == 3)
+            half.append(k)
+        of_tok = []
+        for h, bank in enumerate((T.pa, T.pb)):
+            a = 128 * h
+            need("v", half[h])
+            k = done("v", V.transpose(tt[:, a:a + 128], bank[:, 0:128]))
+            of_tok.append(copy("v", of[:, a:a + 128], tt[:, a:a + 128], k))
+        o_tok = {}
+        for j, pr in enumerate(PAIRS[l]):
+            for d in range(2):
+                a = 32 * order.index(pr[d])
+                o_tok[j] = copy("ssvv"[j], o[:, j, d::2], tab[:].indirect(of[:, a:a + 32]), of_tok[j // 2], ("tb%d" % l, 32))
+        sel = T.sel2 if last else T.sel
+        need("p", k_sel2 if last else k_sel)
+        d_tok = {}
+        for j in (0, 2, 1, 3):
+            need("p", o_tok[j])
+            for u in range(8):
+                d = T["dt%d" % j]
+                d_tok[j] = mm(d[:, u:64:8], o[:, j, 128 * u:128 * u + 128], sel[:, 8 * u:8 * u + 8])
+        ds_ready = []
+        for j in (0, 2, 1, 3):
+            out = T.dsf[:, :, j, :] if last else T["ds%d" % (l + 1)][:, j::4]
+            ds_ready.append(copy("ssvv"[j], out, T["dt%d" % j][:, 0:64], d_tok[j]))
+
+    need("p", k_zf, *ds_ready)
+    half = []
+    for h, bank in enumerate((T.pa, T.pb)):
+        for g2 in range(2):
+            a = (16 if g2 == 0 else 0) + 128 * h
+            k = mm(bank[:, 0:128], T.dsf[:, 4 * g2:4 * g2 + 4, :, :], T.zf[:, a:a + 128], g2 == 0, g2 == 1)
+        half.append(k)
+    for h, bank in enumerate((T.pa, T.pb)):
+        a = 128 * h
+        need("v", half[h])
+        k = done("v", V.transpose(T.yt[:, a:a + 128], bank[:, 0:128]))
+        kk = "ys"[h]
+        need(kk, k)
+        q[kk].dma_start(T.y[:, a:a + 128], T.yt[:, a:a + 128]).then_inc(T.sem["sty%d" % h], 16)
+        need(kk, ("sty%d" % h, 16))
+    need("g", ("qg", cnt["g"]), ("qv", cnt["v"]), ("qs", cnt["s"]), ("qp", cnt["p"]))

@@ -3,27 +3,29 @@ from concourse.mybir import AluOpType, ActivationFunctionType
 
 L = 3
 SCRATCH = {"xt": ("sbuf", [128, 8, 2, 16], "bfloat16"), "xu": ("sbuf", [128, 2, 128], "bfloat16"),
-           "dsf": ("sbuf", [128, 8, 4, 8], "bfloat16"), "lists": ("sbuf", [128, 192], "uint16")}
-for _n, _w in (("xi", 256), ("gw", 6), ("pidx", 2), ("pint", 2)):
+           "dsf": ("sbuf", [128, 8, 4, 8], "bfloat16"), "lists": ("sbuf", [128, 96], "uint16"),
+           "xz0": ("sbuf", [128, 4, 16], "bfloat16"), "xz1": ("sbuf", [128, 4, 16], "bfloat16"),
+           "xzi0": ("sbuf", [128, 4, 16], "float32"), "xzi1": ("sbuf", [128, 4, 16], "float32"),
+           "idy": ("sbuf", [128, 8, 16], "bfloat16"), "iyi": ("sbuf", [128, 8, 16], "float32")}
+for _n, _w in (("xi", 256), ("gi", 3), ("wi", 3), ("pidx", 4), ("pint", 4)):
     SCRATCH[_n] = ("sbuf", [128, _w], "int32")
-for _n, _w in (("gwf", 6), ("pf", 2), ("ki", 128), ("cg", 32), ("cw", 32), ("xzi", 320), ("zi", 288), ("pii", 128),
-               ("sli", 64), ("slj", 64), ("yt", 256)):
+for _n, _w in (("gf", 3), ("wf", 3), ("pf", 4), ("ki", 128), ("cg", 16), ("cw", 16), ("zi", 128),
+               ("si0", 64), ("si1", 64), ("si2", 64), ("yt", 256)):
     SCRATCH[_n] = ("sbuf", [128, _w], "float32")
-for _n, _w in (("xb", 256), ("rep", 128), ("xz", 320), ("z1", 288), ("z64", 288), ("zf", 288), ("pim", 128), ("sel", 64),
-               ("sel2", 64), ("rl", 192)):
+for _n, _w in (("xb", 256), ("rep", 128), ("id1", 128), ("id64", 128), ("sel0", 64), ("sel1", 64), ("sel2", 64), ("rl", 96),
+               ("tab0", 4096), ("tab1", 4096)):
     SCRATCH[_n] = ("sbuf", [128, _w], "bfloat16")
-for _n in ("pa", "pb", "pl", "dt0", "dt1", "dt2", "dt3"):
+for _n in ("pa0", "pa1", "dt00", "dt01", "dt10", "dt11"):
     SCRATCH[_n] = ("psum", [128, 512], "float32")
-SEMAPHORES = ["qg", "qv", "qs", "qp", "ldx", "ldg", "sty0", "sty1"]
+for _n in ("px0", "px1"):
+    SCRATCH[_n] = ("psum", [128, 16, 2, 16], "float32")
+SEMAPHORES = ["qg", "qv", "qs", "qp", "ldx", "ldg", "ldw", "tb0", "tb1", "sty0", "sty1"]
 for _l in range(L):
-    for _n, _w in (("ds", [256]), ("send", [512]), ("land", [512]), ("c", [512]), ("o", [4, 1024]), ("tab", [4096])):
-        SCRATCH["%s%d" % (_n, _l)] = ("sbuf", [128] + _w, "bfloat16")
-    SCRATCH["tt%d" % _l] = ("sbuf", [128, 256], "float32")
-    SCRATCH["of%d" % _l] = ("sbuf", [128, 256], "uint16")
-    SEMAPHORES += ["arr%d" % _l, "sent%d" % _l, "tb%d" % _l]
-
-ORDER = [[0, 1, 4, 5, 2, 3, 6, 7], list(range(8)), list(range(8))]
-PAIRS = [[(0, 4), (1, 5), (2, 6), (3, 7)], [(0, 1), (2, 3), (4, 5), (6, 7)], [(0, 1), (2, 3), (4, 5), (6, 7)]]
+    for _h in range(2):
+        for _n, _w in (("ds", 128), ("send", 256), ("land", 256), ("c", 256), ("o", 2048)):
+            SCRATCH["%s%d%d" % (_n, _l, _h)] = ("sbuf", [128, _w], "bfloat16")
+        SCRATCH["of%d%d" % (_l, _h)] = ("sbuf", [128, 128], "uint16")
+        SEMAPHORES += ["arr%d%d" % (_l, _h), "sent%d%d" % (_l, _h)]
 
 
 def rank_program(g, core, T, topo):
@@ -62,75 +64,74 @@ def rank_program(g, core, T, topo):
         return T.tb[:, l * w:(l + 1) * w]
 
     g.sync.dma_start(T.xi[:], T.x[:]).then_inc(T.sem.ldx, 16)
-    g.scalar.dma_start(T.gw[:, 0:3], T.give[:]).then_inc(T.sem.ldg, 16)
-    g.scalar.dma_start(T.gw[:, 3:6], T.wires[:]).then_inc(T.sem.ldg, 16)
+    g.scalar.dma_start(T.gi[:], T.give[:]).then_inc(T.sem.ldg, 16)
+    g.scalar.dma_start(T.wi[:], T.wires[:]).then_inc(T.sem.ldw, 16)
     g.sync.dma_start(T.tab0[0::2, :], tables(0)).then_inc(T.sem.tb0, 16)
-    g.scalar.dma_start(T.tab0[1::2, :], tables(0)).then_inc(T.sem.tb0, 16)
+    g.scalar.dma_start(T.tab0[1::2, :], tables(1)).then_inc(T.sem.tb0, 16)
 
-    def iota(out, pattern, base, cm):
-        return done("g", g.iota(out[:], pattern, base, cm, allow_small_or_imprecise_dtypes=True))
+    def iota(name, pattern, base, cm):
+        return done("g", g.iota(T[name][:], pattern, base, cm, allow_small_or_imprecise_dtypes=True))
 
-    i_p = done("g", g.iota(T.pidx[:], [[0, 2]], 0, 1))
-    i_k = iota(T.ki, [[0, 8], [1, 4], [0, 4]], 0, 0)
-    i_cg = iota(T.cg, [[1, 32]], 0, 0)
-    i_xz = iota(T.xzi, [[32, 5], [1000, 2], [1, 32]], -1000, -1)
-    i_cw = iota(T.cw, [[2, 4], [8, 4], [1, 2]], 0, 0)
-    i_z = iota(T.zi, [[16, 9], [1000, 2], [1, 16]], -1000, -1)
-    i_s = iota(T.sli, [[2, 8], [16, 8]], 0, -1)
-    i_s2 = iota(T.slj, [[2, 8], [16, 2], [32, 4]], 0, -1)
-    i_pi = iota(T.pii, [[32, 4], [1, 4], [4, 8]], 0, -1)
+    i_p = done("g", g.iota(T.pidx[:], [[0, 4]], 0, 1))
+    i_k = iota("ki", [[0, 8], [1, 8], [0, 2]], 0, 0)
+    i_cg = iota("cg", [[1, 16]], 0, 0)
+    i_xz = [iota("xzi%d" % h, [[32, 4], [1, 8], [8, 2]], 16 * h, -1) for h in range(2)]
+    i_cw = iota("cw", [[1, 2], [2, 8]], 0, 0)
+    i_z = iota("zi", [[1, 128]], 0, -1)
+    i_s = [iota("si%d" % m, [[2, 8], [16, 8]], m, -1) for m in range(2)]
 
     def zeros_of(out, in_, tok):
         need("v", tok)
         return done("v", V.tensor_scalar(out[:], in_[:], 0.0, None, A.is_equal))
 
     need("v", i_p)
-    done("v", V.tensor_scalar(T.pint[:, 0:1], T.pidx[:, 0:1], 3, None, A.bitwise_and))
-    k = done("v", V.tensor_scalar(T.pint[:, 1:2], T.pidx[:, 1:2], 2, None, A.arith_shift_right))
-    k_pf = copy("v", T.pf[:], T.pint[:], k)
-    pm, pd = T.pf[:, 0:1], T.pf[:, 1:2]
+    done("v", V.tensor_scalar(T.pint[:, 0:1], T.pidx[:, 0:1], 7, None, A.bitwise_and))
+    done("v", V.tensor_scalar(T.pint[:, 1:2], T.pidx[:, 1:2], 3, None, A.arith_shift_right))
+    k = done("v", V.tensor_scalar(T.pint[:, 2:3], T.pidx[:, 2:3], 1, None, A.bitwise_and))
+    k_pf = copy("v", T.pf[:, 0:3], T.pint[:, 0:3], k)
+    pm, pd, pt = T.pf[:, 0:1], T.pf[:, 1:2], T.pf[:, 2:3]
     need("v", k_pf, i_k)
     k_rep = done("v", V.tensor_scalar(T.rep[:], T.ki[:], pm, None, A.is_equal))
-    k_xz = zeros_of(T.xz, T.xzi, i_xz)
+    k_xz = [zeros_of(T["xz%d" % h], T["xzi%d" % h], i_xz[h]) for h in range(2)]
 
     def rlist(l, which):
-        a = 64 * l + 32 * which
-        j = 3 * which + l
-        src = T.cw if which else T.cg
-        return done("v", V.tensor_scalar(T.rl[:, a:a + 32], src[:], pd, T.gwf[:, j:j + 1], A.is_equal, A.mult))
+        a = 32 * l + 16 * which
+        src, val = ((T.cg, T.gf), (T.cw, T.wf))[which]
+        return done("v", V.tensor_scalar(T.rl[:, a:a + 16], src[:], pd, val[:, l:l + 1], A.is_equal, A.mult))
+
+    def lists_mm(a, b, tok):
+        need("p", k_rep, tok)
+        return mm(T.pa1[:, a:b], T.rep[:], T.rl[:, a:b])
 
     def lists(a, b, tok):
-        need("p", k_rep, tok)
-        need("v", mm(T.pl[:, a:b], T.rep[:], T.rl[:, a:b]))
-        return done("v", V.tensor_scalar(T.lists[:, a:b], T.pl[:, a:b], 4.0, pm, A.mult, A.add))
+        need("v", tok)
+        return done("v", V.tensor_scalar(T.lists[:, a:b], T.pa1[:, a:b], 2.0, pt, A.mult, A.add))
 
-    k = copy("v", T.gwf[:], T.gw[:], ("ldg", 32))
+    k = copy("v", T.gf[:], T.gi[:], ("ldg", 16))
     need("v", k, i_cg)
-    k_r = rlist(0, 0)
+    k_mm = lists_mm(0, 16, rlist(0, 0))
 
-    for t in range(4):
-        k = copy("v", T.xb[:, t::4], T.xi[:, 64 * t:64 * t + 64], ("ldx", 16))
+    k = copy("v", T.xb[:], T.xi[:], ("ldx", 16))
     need("v", k)
     k_xt = done("v", V.transpose(T.xt[:], T.xb[:]))
     k_u = [copy(k, T.xu[:, j, :], T.xt[:, :, j, :], k_xt) for j, k in enumerate("vs")]
-    k_list = {0: lists(0, 32, k_r)}
-    need("p", k_xz)
-    ds_ready = []
+    k_list = {0: lists(0, 16, k_mm)}
+    need("p", *k_xz)
+    ds_tok = {}
     for h in range(2):
-        for g2 in range(2):
-            a = (32 if g2 == 0 else 0) + 128 * h
-            need("p", k_u[g2])
-            k = mm(T["dt%d" % h][:, 0:128], T.xu[:, g2, :], T.xz[:, a:a + 128], g2 == 0, g2 == 1)
-        ds_ready.append(copy("sv"[h], T.ds0[:, 128 * h:128 * h + 128], T["dt%d" % h][:, 0:128], k))
+        px = T["px%d" % h]
+        for j in range(2):
+            need("p", k_u[j])
+            k = mm(px[:, 0:4, j, :], T.xu[:, j, :], T["xz%d" % h][:])
+        ds_tok[0, h] = [copy("vs"[h], T["ds0%d" % h][:], px[:, 0:4, :, :], k)]
 
-    for l in range(L):
-        ds, send, land, c = T["ds%d" % l], T["send%d" % l], T["land%d" % l], T["c%d" % l]
-        tt, of, o, tab = T["tt%d" % l], T["of%d" % l], T["o%d" % l], T["tab%d" % l]
-        arr, sent = ("arr%d" % l, n - 1), ("sent%d" % l, n - 1)
-        la = 64 * l
-        last = l == L - 1
-        k_sd = [copy(k, send[:, 256 * j:256 * j + 256], ds[:].indirect(T.lists[:, la + 16 * j:la + 16 * j + 16]),
-                     k_list[l], *ds_ready) for j, k in enumerate("vs")]
+    k_wl, k_id, k_sel, own = {}, [], {}, {}
+
+    def lines(l, h):
+        ds, send, land = T["ds%d%d" % (l, h)], T["send%d%d" % (l, h)], T["land%d%d" % (l, h)]
+        a = 32 * l
+        k_sd = [copy(k, send[:, 128 * j:128 * j + 128], ds[:].indirect(T.lists[:, a + 8 * j:a + 8 * j + 8]),
+                     k_list[l], *ds_tok[l, h]) for j, k in enumerate("vs")]
         need("g", *k_sd)
         tr = []
         for j in range(n - 1):
@@ -138,83 +139,96 @@ def rank_program(g, core, T, topo):
             rid, pid = topo.addr(T.cores[r], core)
             eng = topo.engines(core, T.cores[r])
             tr.append(RemoteDMATransfer(dst_ids=[DstId(rid=rid, pnc=pid)], dma_engine_mask=1 << eng[j % len(eng)],
-                                        remote_sem=T.sem["arr%d" % l], src=send[:, 64 * r:64 * r + 64],
-                                        dst=land[:, 64 * rank:64 * rank + 64]))
-        g.remote_dma_fused(tr, local_sem=T.sem["sent%d" % l])
-        k_own = copy("v", land[:, 64 * rank:64 * rank + 64], send[:, 64 * rank:64 * rank + 64], *k_sd)
-        if not last:
-            need("y", sent)
-            for h in range(2):
-                g.sync.dma_start(T["tab%d" % (l + 1)][h::2, :], tables(l + 1)).then_inc(T.sem["tb%d" % (l + 1)], 16)
-        else:
-            need("g", sent)
-        if l == 0:
-            need("v", i_cw)
-            k_wl = {0: lists(32, 64, rlist(0, 1))}
-            k_z1 = zeros_of(T.z1, T.zi, i_z)
-            k_z64 = done("v", V.tensor_scalar(T.z64[:], T.zi[:], 0.0, 64.0, A.is_equal, A.mult))
-            k_sel = zeros_of(T.sel, T.sli, i_s)
-            for m, w in ((1, 0), (1, 1), (2, 0), (2, 1)):
-                k_r = rlist(m, w)
-            k = lists(64, 192, k_r)
-            for m in (1, 2):
-                k_list[m] = k_wl[m] = k
-        elif l == 1:
-            k_sel2 = zeros_of(T.sel2, T.slj, i_s2)
-            need("p", zeros_of(T.pim, T.pii, i_pi))
-            k_zf = copy("s", T.zf[:], T.pl[:, 192:480], mm(T.pl[:, 192:480], T.pim[:], T.z1[:]))
-        k_c = [copy(k, c[:, 256 * j:256 * j + 256], land[:].indirect(T.lists[:, la + 32 + 16 * j:la + 48 + 16 * j]),
-                    arr, k_wl[l], k_own) for j, k in enumerate("vs")]
-        need("p", k_z1, k_z64)
-        order = ORDER[l]
-        w = 2 if l == 0 else 4
-        half = []
-        for h, bank in enumerate((T.pa, T.pb)):
-            for b in range(0, 4, w):
-                for j in range(4):
-                    g2, i = j // 2, j % 2
-                    need("p", k_c[g2])
-                    a = (16 if g2 == 0 else 0) + 32 * order[4 * h + b]
-                    z = T.z1 if i else T.z64
-                    k = mm(bank[:, 32 * b:32 * (b + w)], c[:, 128 * j:128 * j + 128], z[:, a:a + 32 * w], j == 0, j == 3)
-            half.append(k)
-        of_tok = []
-        for h, bank in enumerate((T.pa, T.pb)):
-            a = 128 * h
-            need("v", half[h])
-            k = done("v", V.transpose(tt[:, a:a + 128], bank[:, 0:128]))
-            of_tok.append(copy("v", of[:, a:a + 128], tt[:, a:a + 128], k))
-        o_tok = {}
-        for j, pr in enumerate(PAIRS[l]):
-            for d in range(2):
-                a = 32 * order.index(pr[d])
-                o_tok[j] = copy("ssvv"[j], o[:, j, d::2], tab[:].indirect(of[:, a:a + 32]), of_tok[j // 2], ("tb%d" % l, 32))
-        sel = T.sel2 if last else T.sel
-        need("p", k_sel2 if last else k_sel)
-        d_tok = {}
-        for j in (0, 2, 1, 3):
-            need("p", o_tok[j])
-            for u in range(8):
-                d = T["dt%d" % j]
-                d_tok[j] = mm(d[:, u:64:8], o[:, j, 128 * u:128 * u + 128], sel[:, 8 * u:8 * u + 8])
-        ds_ready = []
-        for j in (0, 2, 1, 3):
-            out = T.dsf[:, :, j, :] if last else T["ds%d" % (l + 1)][:, j::4]
-            ds_ready.append(copy("ssvv"[j], out, T["dt%d" % j][:, 0:64], d_tok[j]))
+                                        remote_sem=T.sem["arr%d%d" % (l, h)], src=send[:, 32 * r:32 * r + 32],
+                                        dst=land[:, 32 * rank:32 * rank + 32]))
+        g.remote_dma_fused(tr, local_sem=T.sem["sent%d%d" % (l, h)])
+        own[l, h] = copy("s", land[:, 32 * rank:32 * rank + 32], send[:, 32 * rank:32 * rank + 32], *k_sd)
 
-    need("p", k_zf, *ds_ready)
-    half = []
-    for h, bank in enumerate((T.pa, T.pb)):
-        for g2 in range(2):
-            a = (16 if g2 == 0 else 0) + 128 * h
-            k = mm(bank[:, 0:128], T.dsf[:, 4 * g2:4 * g2 + 4, :, :], T.zf[:, a:a + 128], g2 == 0, g2 == 1)
-        half.append(k)
-    for h, bank in enumerate((T.pa, T.pb)):
+    k_c, of_tok, o_tok, d_tok = {}, {}, {}, {}
+
+    def inputs(l, h):
+        land, c = T["land%d%d" % (l, h)], T["c%d%d" % (l, h)]
+        a = 32 * l + 16
+        k_c[l, h] = [copy(k, c[:, 128 * j:128 * j + 128], land[:].indirect(T.lists[:, a + 8 * j:a + 8 * j + 8]),
+                          ("arr%d%d" % (l, h), n - 1), k_wl[l], own[l, h]) for j, k in enumerate("vs")]
+
+    def addresses(l, h):
+        c, pa = T["c%d%d" % (l, h)], T["pa%d" % h]
+        need("p", *k_id)
+        need("p", k_c[l, h][0])
+        mm(pa[:, 0:128], c[:, 0:128], T.id64[:], True, False)
+        need("p", k_c[l, h][1])
+        of_tok[l, h] = mm(pa[:, 0:128], c[:, 128:256], T.id1[:], False, True)
+
+    def lookups(l, h):
+        tab, of, o = T["tab%d" % (l // 2)], T["of%d%d" % (l, h)], T["o%d%d" % (l, h)]
+        k_of = copy("v", of[:], T["pa%d" % h][:, 0:128], of_tok[l, h])
+        o_tok[l, h] = [copy(k, o[:, 1024 * j:1024 * j + 1024], tab[:].indirect(of[:, 64 * j:64 * j + 64]), k_of,
+                            ("tb%d" % (l // 2), 32)) for j, k in enumerate("vs")]
+
+    def pick(l, h):
+        o, sel = T["o%d%d" % (l, h)], T["sel%d" % l]
+        need("p", k_sel[l], *o_tok[l, h])
+        for t in range(2):
+            for u in range(8):
+                d_tok[l, h, t] = mm(T["dt%d%d" % (h, t)][:, u:64:8], o[:, 2 * u + t::16], sel[:, 8 * u:8 * u + 8])
+
+    def codes(l, h):
+        out = []
+        for t, k in enumerate("vs"):
+            dst = T.dsf[:, :, 2 * h + t, :] if l == L - 1 else T["ds%d%d" % (l + 1, h)][:, t::2]
+            out.append(copy(k, dst, T["dt%d%d" % (h, t)][:, 0:64], d_tok[l, h, t]))
+        ds_tok[l + 1, h] = out
+        if l < L - 1:
+            lines(l + 1, h)
+
+    for h in range(2):
+        lines(0, h)
+    need("y", ("sent00", n - 1), ("sent01", n - 1))
+    for j in range(2):
+        g.sync.dma_start(T.tab1[j::2, :], tables(2)).then_inc(T.sem.tb1, 16)
+    i_iy = iota("iyi", [[1, 128]], 0, -1)
+    i_s2 = iota("si2", [[2, 8], [16, 2], [32, 4]], 0, -1)
+    k = copy("v", T.wf[:], T.wi[:], ("ldw", 16))
+    need("v", k, i_cw)
+    k_wl[0] = lists(16, 32, lists_mm(16, 32, rlist(0, 1)))
+    k_id.append(zeros_of(T.id1, T.zi, i_z))
+    k_id.append(done("v", V.tensor_scalar(T.id64[:], T.zi[:], 0.0, 64.0, A.is_equal, A.mult)))
+    for m in range(2):
+        k_sel[m] = zeros_of(T["sel%d" % m], T["si%d" % m], i_s[m])
+    for m, w in ((1, 0), (1, 1), (2, 0), (2, 1)):
+        k = rlist(m, w)
+    k = lists(32, 96, lists_mm(32, 96, k))
+    for m in (1, 2):
+        k_list[m] = k_wl[m] = k
+    k_sel[2] = zeros_of(T.sel2, T.si2, i_s2)
+    k_iy = zeros_of(T.idy, T.iyi, i_iy)
+
+    for l in range(L):
+        inputs(l, 0)
+        addresses(l, 0)
+        lookups(l, 0)
+        inputs(l, 1)
+        pick(l, 0)
+        addresses(l, 1)
+        codes(l, 0)
+        lookups(l, 1)
+        pick(l, 1)
+        codes(l, 1)
+
+    need("p", k_iy, *ds_tok[L, 0])
+    need("p", *ds_tok[L, 1])
+    for j in range(2):
+        k = mm(T.px0[:, 0:8, j, :], T.dsf[:, 4 * j:4 * j + 4, :, :], T.idy[:])
+    need("v", k)
+    for h in range(2):
         a = 128 * h
-        need("v", half[h])
-        k = done("v", V.transpose(T.yt[:, a:a + 128], bank[:, 0:128]))
+        k = done("v", V.transpose(T.yt[:, a:a + 128], T.px0[:, 4 * h:4 * h + 4, :, :]))
         kk = "ys"[h]
         need(kk, k)
         q[kk].dma_start(T.y[:, a:a + 128], T.yt[:, a:a + 128]).then_inc(T.sem["sty%d" % h], 16)
         need(kk, ("sty%d" % h, 16))
+    for l in range(L):
+        for h in range(2):
+            need("g", ("sent%d%d" % (l, h), n - 1))
     need("g", ("qg", cnt["g"]), ("qv", cnt["v"]), ("qs", cnt["s"]), ("qp", cnt["p"]))

@@ -2,24 +2,18 @@ from concourse.bass import DstId, RemoteDMATransfer
 from concourse.mybir import AluOpType, ActivationFunctionType
 
 L = 3
-SCRATCH = {"xt": ("sbuf", [128, 8, 2, 16], "bfloat16"), "xu": ("sbuf", [128, 2, 128], "bfloat16"),
-           "dsf": ("sbuf", [128, 8, 4, 8], "bfloat16"), "lists": ("sbuf", [128, 96], "uint16"),
-           "xz0": ("sbuf", [128, 4, 16], "bfloat16"), "xz1": ("sbuf", [128, 4, 16], "bfloat16"),
-           "xzi0": ("sbuf", [128, 4, 16], "float32"), "xzi1": ("sbuf", [128, 4, 16], "float32"),
-           "idy": ("sbuf", [128, 8, 16], "bfloat16"), "iyi": ("sbuf", [128, 8, 16], "float32")}
-for _n, _w in (("xi", 256), ("gi", 3), ("wi", 3), ("pidx", 4), ("pint", 4)):
+SCRATCH = {"xs": ("sbuf", [128, 256], "int32"), "yt": ("sbuf", [128, 8, 32], "float32"),
+           "lists": ("sbuf", [128, 96], "uint16")}
+for _n, _w in (("gi", 3), ("wi", 3), ("pidx", 4), ("pint", 4), ("gsh", 4)):
     SCRATCH[_n] = ("sbuf", [128, _w], "int32")
-for _n, _w in (("gf", 3), ("wf", 3), ("pf", 4), ("ki", 128), ("cg", 16), ("cw", 16), ("zi", 128),
-               ("si0", 64), ("si1", 64), ("si2", 64), ("yt", 256)):
+for _n, _w in (("g0", 4), ("gf", 4), ("wf", 4), ("pf", 4), ("ki", 128), ("cg", 16), ("cw", 16), ("gm", 16), ("wm", 16),
+               ("zi", 128)):
     SCRATCH[_n] = ("sbuf", [128, _w], "float32")
-for _n, _w in (("xb", 256), ("rep", 128), ("id1", 128), ("id64", 128), ("sel0", 64), ("sel1", 64), ("sel2", 64), ("rl", 96),
-               ("tab0", 4096), ("tab1", 4096)):
+for _n, _w in (("rep", 128), ("id1", 128), ("id64", 128), ("rl", 96), ("tab0", 4096), ("tab1", 4096)):
     SCRATCH[_n] = ("sbuf", [128, _w], "bfloat16")
-for _n in ("pa0", "pa1", "dt00", "dt01", "dt10", "dt11"):
+for _n in ("pa0", "pa1", "pl", "dt00", "dt01", "dt10", "dt11"):
     SCRATCH[_n] = ("psum", [128, 512], "float32")
-for _n in ("px0", "px1"):
-    SCRATCH[_n] = ("psum", [128, 16, 2, 16], "float32")
-SEMAPHORES = ["qg", "qv", "qs", "qp", "ldx", "ldg", "ldw", "tb0", "tb1", "sty0", "sty1"]
+SEMAPHORES = ["qg", "qv", "qs", "qp", "ldx", "ldg", "ldw", "tb0", "tb1", "sty"]
 for _l in range(L):
     for _h in range(2):
         for _n, _w in (("ds", 128), ("send", 256), ("land", 256), ("c", 256), ("o", 2048)):
@@ -59,79 +53,67 @@ def rank_program(g, core, T, topo):
             return done("v", V.tensor_copy(out, in_))
         return done("s", g.scalar.activation(out, in_, ActivationFunctionType.Copy))
 
+    def times(out, in_, scale, *toks):
+        need("s", *toks)
+        return done("s", g.scalar.activation(out, in_, ActivationFunctionType.Copy, 0.0, scale))
+
+    def ts(out, in0, *args):
+        return done("v", V.tensor_scalar(out, in0, *args))
+
     def tables(l):
         w = 8 * 4096
         return T.tb[:, l * w:(l + 1) * w]
 
-    g.sync.dma_start(T.xi[:], T.x[:]).then_inc(T.sem.ldx, 16)
     g.scalar.dma_start(T.gi[:], T.give[:]).then_inc(T.sem.ldg, 16)
-    g.scalar.dma_start(T.wi[:], T.wires[:]).then_inc(T.sem.ldw, 16)
+    for a in range(8):
+        q["ys"[a % 2]].dma_start(T.xs[:, 32 * a:32 * a + 32], T.x[16 * a:16 * a + 16, :]).then_inc(T.sem.ldx, 16)
+    g.sync.dma_start(T.wi[:], T.wires[:]).then_inc(T.sem.ldw, 16)
     g.sync.dma_start(T.tab0[0::2, :], tables(0)).then_inc(T.sem.tb0, 16)
     g.scalar.dma_start(T.tab0[1::2, :], tables(1)).then_inc(T.sem.tb0, 16)
 
-    def iota(name, pattern, base, cm):
-        return done("g", g.iota(T[name][:], pattern, base, cm, allow_small_or_imprecise_dtypes=True))
+    def iota(name, pattern, cm):
+        return done("g", g.iota(T[name][:], pattern, 0, cm, allow_small_or_imprecise_dtypes=True))
 
     i_p = done("g", g.iota(T.pidx[:], [[0, 4]], 0, 1))
-    i_k = iota("ki", [[0, 8], [1, 8], [0, 2]], 0, 0)
-    i_cg = iota("cg", [[1, 16]], 0, 0)
-    i_xz = [iota("xzi%d" % h, [[32, 4], [1, 8], [8, 2]], 16 * h, -1) for h in range(2)]
-    i_cw = iota("cw", [[1, 2], [2, 8]], 0, 0)
-    i_z = iota("zi", [[1, 128]], 0, -1)
-    i_s = [iota("si%d" % m, [[2, 8], [16, 8]], m, -1) for m in range(2)]
-
-    def zeros_of(out, in_, tok):
-        need("v", tok)
-        return done("v", V.tensor_scalar(out[:], in_[:], 0.0, None, A.is_equal))
+    i_k = iota("ki", [[0, 8], [1, 8], [0, 2]], 0)
+    i_cg = iota("cg", [[1, 16]], 0)
+    i_cw = iota("cw", [[1, 2], [2, 8]], 0)
+    i_z = iota("zi", [[1, 128]], -1)
 
     need("v", i_p)
-    done("v", V.tensor_scalar(T.pint[:, 0:1], T.pidx[:, 0:1], 7, None, A.bitwise_and))
-    done("v", V.tensor_scalar(T.pint[:, 1:2], T.pidx[:, 1:2], 3, None, A.arith_shift_right))
-    k = done("v", V.tensor_scalar(T.pint[:, 2:3], T.pidx[:, 2:3], 1, None, A.bitwise_and))
+    ts(T.pint[:, 0:1], T.pidx[:, 0:1], 7, None, A.bitwise_and)
+    ts(T.pint[:, 1:2], T.pidx[:, 1:2], 3, None, A.arith_shift_right)
+    k = ts(T.pint[:, 2:3], T.pidx[:, 2:3], 1, None, A.bitwise_and)
     k_pf = copy("v", T.pf[:, 0:3], T.pint[:, 0:3], k)
     pm, pd, pt = T.pf[:, 0:1], T.pf[:, 1:2], T.pf[:, 2:3]
     need("v", k_pf, i_k)
-    k_rep = done("v", V.tensor_scalar(T.rep[:], T.ki[:], pm, None, A.is_equal))
-    k_xz = [zeros_of(T["xz%d" % h], T["xzi%d" % h], i_xz[h]) for h in range(2)]
+    k_rep = ts(T.rep[:], T.ki[:], pm, None, A.is_equal)
 
-    def rlist(l, which):
-        a = 32 * l + 16 * which
-        src, val = ((T.cg, T.gf), (T.cw, T.wf))[which]
-        return done("v", V.tensor_scalar(T.rl[:, a:a + 16], src[:], pd, val[:, l:l + 1], A.is_equal, A.mult))
+    def lists_mm(a, b, *toks):
+        need("p", k_rep, *toks)
+        return mm(T.pl[:, a:b], T.rep[:], T.rl[:, a:b])
 
-    def lists_mm(a, b, tok):
-        need("p", k_rep, tok)
-        return mm(T.pa1[:, a:b], T.rep[:], T.rl[:, a:b])
-
-    def lists(a, b, tok):
-        need("v", tok)
-        return done("v", V.tensor_scalar(T.lists[:, a:b], T.pa1[:, a:b], 2.0, pt, A.mult, A.add))
-
-    k = copy("v", T.gf[:], T.gi[:], ("ldg", 16))
-    need("v", k, i_cg)
-    k_mm = lists_mm(0, 16, rlist(0, 0))
-
-    k = copy("v", T.xb[:], T.xi[:], ("ldx", 16))
+    need("v", ("ldg", 16))
+    ts(T.g0[:, 0:1], T.gi[:, 0:1], 0.125, None, A.mult)
+    k = ts(T.gsh[:, 0:1], T.gi[:, 0:1], 3, None, A.arith_shift_right)
     need("v", k)
-    k_xt = done("v", V.transpose(T.xt[:], T.xb[:]))
-    k_u = [copy(k, T.xu[:, j, :], T.xt[:, :, j, :], k_xt) for j, k in enumerate("vs")]
-    k_list = {0: lists(0, 16, k_mm)}
-    need("p", *k_xz)
-    ds_tok = {}
-    for h in range(2):
-        px = T["px%d" % h]
-        for j in range(2):
-            need("p", k_u[j])
-            k = mm(px[:, 0:4, j, :], T.xu[:, j, :], T["xz%d" % h][:])
-        ds_tok[0, h] = [copy("vs"[h], T["ds0%d" % h][:], px[:, 0:4, :, :], k)]
+    k = ts(T.g0[:, 1:2], T.gsh[:, 0:1], 3.0, T.g0[:, 0:1], A.mult, A.add)
+    need("v", k, i_cg)
+    k = lists_mm(0, 16, ts(T.rl[:, 0:16], T.cg[:], pd, T.g0[:, 1:2], A.is_equal, A.mult))
+    need("v", k)
+    k_list = {0: ts(T.lists[:, 0:16], T.pl[:, 0:16], pt, 8.0, A.add, A.mult)}
 
-    k_wl, k_id, k_sel, own = {}, [], {}, {}
+    k_wl, own, ds_tok = {}, {}, {}
 
     def lines(l, h):
-        ds, send, land = T["ds%d%d" % (l, h)], T["send%d%d" % (l, h)], T["land%d%d" % (l, h)]
-        a = 32 * l
-        k_sd = [copy(k, send[:, 128 * j:128 * j + 128], ds[:].indirect(T.lists[:, a + 8 * j:a + 8 * j + 8]),
-                     k_list[l], *ds_tok[l, h]) for j, k in enumerate("vs")]
+        send, land, a = T["send%d%d" % (l, h)], T["land%d%d" % (l, h)], 32 * l
+        if l == 0:
+            need("v", ("ldx", 128))
+            k_sd = [copy("v", send[:], T.xs[:, 16 * h:256].indirect(T.lists[:, 0:16]), k_list[0])]
+        else:
+            ds = T["ds%d%d" % (l, h)]
+            k_sd = [copy(k, send[:, 128 * j:128 * j + 128], ds[:].indirect(T.lists[:, a + 8 * j:a + 8 * j + 8]),
+                         k_list[l], *ds_tok[l, h]) for j, k in enumerate("vs")]
         need("g", *k_sd)
         tr = []
         for j in range(n - 1):
@@ -142,7 +124,10 @@ def rank_program(g, core, T, topo):
                                         remote_sem=T.sem["arr%d%d" % (l, h)], src=send[:, 32 * r:32 * r + 32],
                                         dst=land[:, 32 * rank:32 * rank + 32]))
         g.remote_dma_fused(tr, local_sem=T.sem["sent%d%d" % (l, h)])
-        own[l, h] = copy("s", land[:, 32 * rank:32 * rank + 32], send[:, 32 * rank:32 * rank + 32], *k_sd)
+
+    def own_lines(l, h):
+        send, land, b = T["send%d%d" % (l, h)], T["land%d%d" % (l, h)], 32 * rank
+        own[l, h] = done("g", g.affine_select(land[:, b:b + 32], send[:, b:b + 32], [[0, 32]], A.is_ge, 0.0, 0, 0))
 
     k_c, of_tok, o_tok, d_tok = {}, {}, {}, {}
 
@@ -150,7 +135,7 @@ def rank_program(g, core, T, topo):
         land, c = T["land%d%d" % (l, h)], T["c%d%d" % (l, h)]
         a = 32 * l + 16
         k_c[l, h] = [copy(k, c[:, 128 * j:128 * j + 128], land[:].indirect(T.lists[:, a + 8 * j:a + 8 * j + 8]),
-                          ("arr%d%d" % (l, h), n - 1), k_wl[l], own[l, h]) for j, k in enumerate("vs")]
+                          k_wl[l], own[l, h], ("arr%d%d" % (l, h), n - 1)) for j, k in enumerate("vs")]
 
     def addresses(l, h):
         c, pa = T["c%d%d" % (l, h)], T["pa%d" % h]
@@ -167,42 +152,48 @@ def rank_program(g, core, T, topo):
                             ("tb%d" % (l // 2), 32)) for j, k in enumerate("vs")]
 
     def pick(l, h):
-        o, sel = T["o%d%d" % (l, h)], T["sel%d" % l]
-        need("p", k_sel[l], *o_tok[l, h])
+        o = T["o%d%d" % (l, h)]
+        need("p", *o_tok[l, h])
         for t in range(2):
             for u in range(8):
-                d_tok[l, h, t] = mm(T["dt%d%d" % (h, t)][:, u:64:8], o[:, 2 * u + t::16], sel[:, 8 * u:8 * u + 8])
+                d_tok[l, h, t] = mm(T["dt%d%d" % (h, t)][:, u:64:8], o[:, 2 * u + t::16], T.id1[:, 2 * u + l % 2::16])
 
     def codes(l, h):
         out = []
         for t, k in enumerate("vs"):
-            dst = T.dsf[:, :, 2 * h + t, :] if l == L - 1 else T["ds%d%d" % (l + 1, h)][:, t::2]
+            b = 16 * h + 8 * t
+            dst = T.yt[:, :, b:b + 8] if l == L - 1 else T["ds%d%d" % (l + 1, h)][:, t::2]
             out.append(copy(k, dst, T["dt%d%d" % (h, t)][:, 0:64], d_tok[l, h, t]))
         ds_tok[l + 1, h] = out
         if l < L - 1:
             lines(l + 1, h)
+            own_lines(l + 1, h)
 
     for h in range(2):
         lines(0, h)
+    for h in range(2):
+        own_lines(0, h)
     need("y", ("sent00", n - 1), ("sent01", n - 1))
     for j in range(2):
         g.sync.dma_start(T.tab1[j::2, :], tables(2)).then_inc(T.sem.tb1, 16)
-    i_iy = iota("iyi", [[1, 128]], 0, -1)
-    i_s2 = iota("si2", [[2, 8], [16, 2], [32, 4]], 0, -1)
-    k = copy("v", T.wf[:], T.wi[:], ("ldw", 16))
-    need("v", k, i_cw)
-    k_wl[0] = lists(16, 32, lists_mm(16, 32, rlist(0, 1)))
-    k_id.append(zeros_of(T.id1, T.zi, i_z))
-    k_id.append(done("v", V.tensor_scalar(T.id64[:], T.zi[:], 0.0, 64.0, A.is_equal, A.mult)))
-    for m in range(2):
-        k_sel[m] = zeros_of(T["sel%d" % m], T["si%d" % m], i_s[m])
-    for m, w in ((1, 0), (1, 1), (2, 0), (2, 1)):
-        k = rlist(m, w)
-    k = lists(32, 96, lists_mm(32, 96, k))
-    for m in (1, 2):
-        k_list[m] = k_wl[m] = k
-    k_sel[2] = zeros_of(T.sel2, T.si2, i_s2)
-    k_iy = zeros_of(T.idy, T.iyi, i_iy)
+
+    k_wf = copy("v", T.wf[:, 0:3], T.wi[:], ("ldw", 16))
+    need("v", i_cw)
+    k_wm = ts(T.wm[:], T.cw[:], pd, None, A.is_equal)
+    k_gf = copy("v", T.gf[:, 0:3], T.gi[:])
+    k_gm = ts(T.gm[:], T.cg[:], pd, None, A.is_equal)
+    need("v", i_z)
+    k_id = [ts(T.id1[:], T.zi[:], 0.0, None, A.is_equal)]
+    for l in range(L):
+        a = 32 * l + 16
+        k = times(T.rl[:, a:a + 16], T.wm[:], T.wf[:, l:l + 1], k_wf, k_wm)
+    for l in (1, 2):
+        a = 32 * l
+        k = times(T.rl[:, a:a + 16], T.gm[:], T.gf[:, l:l + 1], k_gf, k_gm)
+    k_id.append(times(T.id64[:], T.id1[:], 64.0, k_id[0]))
+    k = lists_mm(16, 96, k, k_list[0])
+    need("v", k)
+    k_list[1] = k_list[2] = k_wl[0] = k_wl[1] = k_wl[2] = ts(T.lists[:, 16:96], T.pl[:, 16:96], 2.0, pt, A.mult, A.add)
 
     for l in range(L):
         inputs(l, 0)
@@ -216,19 +207,11 @@ def rank_program(g, core, T, topo):
         pick(l, 1)
         codes(l, 1)
 
-    need("p", k_iy, *ds_tok[L, 0])
-    need("p", *ds_tok[L, 1])
-    for j in range(2):
-        k = mm(T.px0[:, 0:8, j, :], T.dsf[:, 4 * j:4 * j + 4, :, :], T.idy[:])
-    need("v", k)
-    for h in range(2):
-        a = 128 * h
-        k = done("v", V.transpose(T.yt[:, a:a + 128], T.px0[:, 4 * h:4 * h + 4, :, :]))
-        kk = "ys"[h]
-        need(kk, k)
-        q[kk].dma_start(T.y[:, a:a + 128], T.yt[:, a:a + 128]).then_inc(T.sem["sty%d" % h], 16)
-        need(kk, ("sty%d" % h, 16))
+    for k in "ys":
+        need(k, *ds_tok[L, 0], *ds_tok[L, 1])
+    for a in range(8):
+        q["ys"[a % 2]].dma_start(T.y[16 * a:16 * a + 16, :], T.yt[:, a, :]).then_inc(T.sem.sty, 16)
     for l in range(L):
         for h in range(2):
             need("g", ("sent%d%d" % (l, h), n - 1))
-    need("g", ("qg", cnt["g"]), ("qv", cnt["v"]), ("qs", cnt["s"]), ("qp", cnt["p"]))
+    need("g", ("sty", 128), ("qg", cnt["g"]), ("qv", cnt["v"]), ("qs", cnt["s"]), ("qp", cnt["p"]))

from concourse.bass import DstId, RemoteDMATransfer
from concourse.mybir import AluOpType, ActivationFunctionType

L = 3
SCRATCH = {"xs": ("sbuf", [128, 256], "int32"), "yt": ("sbuf", [128, 8, 32], "float32"),
           "lists": ("sbuf", [128, 96], "uint16")}
for _n, _w in (("gi", 3), ("wi", 3), ("pidx", 4), ("pint", 4), ("gsh", 4)):
    SCRATCH[_n] = ("sbuf", [128, _w], "int32")
for _n, _w in (("g0", 4), ("gf", 4), ("wf", 4), ("pf", 4), ("ki", 128), ("cg", 16), ("cw", 16), ("gm", 16), ("wm", 16),
               ("zi", 128)):
    SCRATCH[_n] = ("sbuf", [128, _w], "float32")
for _n, _w in (("rep", 128), ("id1", 128), ("id64", 128), ("rl", 96), ("tab0", 4096), ("tab1", 4096)):
    SCRATCH[_n] = ("sbuf", [128, _w], "bfloat16")
for _n in ("pa0", "pa1", "pl", "dt00", "dt01", "dt10", "dt11"):
    SCRATCH[_n] = ("psum", [128, 512], "float32")
SEMAPHORES = ["qg", "qv", "qs", "qp", "ldx", "ldg", "ldw", "tb0", "tb1", "sty"]
for _l in range(L):
    for _h in range(2):
        for _n, _w in (("ds", 128), ("send", 256), ("land", 256), ("c", 256), ("o", 2048)):
            SCRATCH["%s%d%d" % (_n, _l, _h)] = ("sbuf", [128, _w], "bfloat16")
        SCRATCH["of%d%d" % (_l, _h)] = ("sbuf", [128, 128], "uint16")
        SEMAPHORES += ["arr%d%d" % (_l, _h), "sent%d%d" % (_l, _h)]


def rank_program(g, core, T, topo):
    rank = T.rank_of(core)
    if rank is None:
        return
    A = AluOpType
    n = len(T.cores)
    q = {"g": g, "v": g.vector, "s": g.scalar, "p": g.tensor, "y": g.sync}
    cnt = {"g": 0, "v": 0, "s": 0, "p": 0}
    seen = {}
    V = g.vector

    def done(k, instr):
        cnt[k] += 1
        instr.then_inc(T.sem["q" + k], 1)
        return ("q" + k, cnt[k])

    def need(k, *toks):
        for sem, val in toks:
            if seen.get((k, sem), 0) < val:
                q[k].wait_ge(T.sem[sem], val)
                seen[(k, sem)] = val

    def mm(out, lhsT, rhs, start=True, stop=True):
        return done("p", g.tensor.matmul(out, lhsT, rhs, start, stop))

    def copy(k, out, in_, *toks):
        need(k, *toks)
        if k == "v":
            return done("v", V.tensor_copy(out, in_))
        return done("s", g.scalar.activation(out, in_, ActivationFunctionType.Copy))

    def times(out, in_, scale, *toks):
        need("s", *toks)
        return done("s", g.scalar.activation(out, in_, ActivationFunctionType.Copy, 0.0, scale))

    def ts(out, in0, *args):
        return done("v", V.tensor_scalar(out, in0, *args))

    def tables(l):
        w = 8 * 4096
        return T.tb[:, l * w:(l + 1) * w]

    g.scalar.dma_start(T.gi[:], T.give[:]).then_inc(T.sem.ldg, 16)
    for a in range(8):
        q["ys"[a % 2]].dma_start(T.xs[:, 32 * a:32 * a + 32], T.x[16 * a:16 * a + 16, :]).then_inc(T.sem.ldx, 16)
    g.sync.dma_start(T.wi[:], T.wires[:]).then_inc(T.sem.ldw, 16)
    g.sync.dma_start(T.tab0[0::2, :], tables(0)).then_inc(T.sem.tb0, 16)
    g.scalar.dma_start(T.tab0[1::2, :], tables(1)).then_inc(T.sem.tb0, 16)

    def iota(name, pattern, cm):
        return done("g", g.iota(T[name][:], pattern, 0, cm, allow_small_or_imprecise_dtypes=True))

    i_p = done("g", g.iota(T.pidx[:], [[0, 4]], 0, 1))
    i_k = iota("ki", [[0, 8], [1, 8], [0, 2]], 0)
    i_cg = iota("cg", [[1, 16]], 0)
    i_cw = iota("cw", [[1, 2], [2, 8]], 0)
    i_z = iota("zi", [[1, 128]], -1)

    need("v", i_p)
    ts(T.pint[:, 0:1], T.pidx[:, 0:1], 7, None, A.bitwise_and)
    ts(T.pint[:, 1:2], T.pidx[:, 1:2], 3, None, A.arith_shift_right)
    k = ts(T.pint[:, 2:3], T.pidx[:, 2:3], 1, None, A.bitwise_and)
    k_pf = copy("v", T.pf[:, 0:3], T.pint[:, 0:3], k)
    pm, pd, pt = T.pf[:, 0:1], T.pf[:, 1:2], T.pf[:, 2:3]
    need("v", k_pf, i_k)
    k_rep = ts(T.rep[:], T.ki[:], pm, None, A.is_equal)

    def lists_mm(a, b, *toks):
        need("p", k_rep, *toks)
        return mm(T.pl[:, a:b], T.rep[:], T.rl[:, a:b])

    need("v", ("ldg", 16))
    ts(T.g0[:, 0:1], T.gi[:, 0:1], 0.125, None, A.mult)
    k = ts(T.gsh[:, 0:1], T.gi[:, 0:1], 3, None, A.arith_shift_right)
    need("v", k)
    k = ts(T.g0[:, 1:2], T.gsh[:, 0:1], 3.0, T.g0[:, 0:1], A.mult, A.add)
    need("v", k, i_cg)
    k = lists_mm(0, 16, ts(T.rl[:, 0:16], T.cg[:], pd, T.g0[:, 1:2], A.is_equal, A.mult))
    need("v", k)
    k_list = {0: ts(T.lists[:, 0:16], T.pl[:, 0:16], pt, 8.0, A.add, A.mult)}

    k_wl, own, ds_tok = {}, {}, {}

    def lines(l, h):
        send, land, a = T["send%d%d" % (l, h)], T["land%d%d" % (l, h)], 32 * l
        if l == 0:
            need("v", ("ldx", 128))
            k_sd = [copy("v", send[:], T.xs[:, 16 * h:256].indirect(T.lists[:, 0:16]), k_list[0])]
        else:
            ds = T["ds%d%d" % (l, h)]
            k_sd = [copy(k, send[:, 128 * j:128 * j + 128], ds[:].indirect(T.lists[:, a + 8 * j:a + 8 * j + 8]),
                         k_list[l], *ds_tok[l, h]) for j, k in enumerate("vs")]
        need("g", *k_sd)
        tr = []
        for j in range(n - 1):
            r = (rank + 1 + j) % n
            rid, pid = topo.addr(T.cores[r], core)
            eng = topo.engines(core, T.cores[r])
            tr.append(RemoteDMATransfer(dst_ids=[DstId(rid=rid, pnc=pid)], dma_engine_mask=1 << eng[j % len(eng)],
                                        remote_sem=T.sem["arr%d%d" % (l, h)], src=send[:, 32 * r:32 * r + 32],
                                        dst=land[:, 32 * rank:32 * rank + 32]))
        g.remote_dma_fused(tr, local_sem=T.sem["sent%d%d" % (l, h)])

    def own_lines(l, h):
        send, land, b = T["send%d%d" % (l, h)], T["land%d%d" % (l, h)], 32 * rank
        own[l, h] = done("g", g.affine_select(land[:, b:b + 32], send[:, b:b + 32], [[0, 32]], A.is_ge, 0.0, 0, 0))

    k_c, of_tok, o_tok, d_tok = {}, {}, {}, {}

    def inputs(l, h):
        land, c = T["land%d%d" % (l, h)], T["c%d%d" % (l, h)]
        a = 32 * l + 16
        k_c[l, h] = [copy(k, c[:, 128 * j:128 * j + 128], land[:].indirect(T.lists[:, a + 8 * j:a + 8 * j + 8]),
                          k_wl[l], own[l, h], ("arr%d%d" % (l, h), n - 1)) for j, k in enumerate("vs")]

    def addresses(l, h):
        c, pa = T["c%d%d" % (l, h)], T["pa%d" % h]
        need("p", *k_id)
        need("p", k_c[l, h][0])
        mm(pa[:, 0:128], c[:, 0:128], T.id64[:], True, False)
        need("p", k_c[l, h][1])
        of_tok[l, h] = mm(pa[:, 0:128], c[:, 128:256], T.id1[:], False, True)

    def lookups(l, h):
        tab, of, o = T["tab%d" % (l // 2)], T["of%d%d" % (l, h)], T["o%d%d" % (l, h)]
        k_of = copy("v", of[:], T["pa%d" % h][:, 0:128], of_tok[l, h])
        o_tok[l, h] = [copy(k, o[:, 1024 * j:1024 * j + 1024], tab[:].indirect(of[:, 64 * j:64 * j + 64]), k_of,
                            ("tb%d" % (l // 2), 32)) for j, k in enumerate("vs")]

    def pick(l, h):
        o = T["o%d%d" % (l, h)]
        need("p", *o_tok[l, h])
        for t in range(2):
            for u in range(8):
                d_tok[l, h, t] = mm(T["dt%d%d" % (h, t)][:, u:64:8], o[:, 2 * u + t::16], T.id1[:, 2 * u + l % 2::16])

    def codes(l, h):
        out = []
        for t, k in enumerate("vs"):
            b = 16 * h + 8 * t
            dst = T.yt[:, :, b:b + 8] if l == L - 1 else T["ds%d%d" % (l + 1, h)][:, t::2]
            out.append(copy(k, dst, T["dt%d%d" % (h, t)][:, 0:64], d_tok[l, h, t]))
        ds_tok[l + 1, h] = out
        if l < L - 1:
            lines(l + 1, h)
            own_lines(l + 1, h)

    for h in range(2):
        lines(0, h)
    for h in range(2):
        own_lines(0, h)
    need("y", ("sent00", n - 1), ("sent01", n - 1))
    for j in range(2):
        g.sync.dma_start(T.tab1[j::2, :], tables(2)).then_inc(T.sem.tb1, 16)

    k_wf = copy("v", T.wf[:, 0:3], T.wi[:], ("ldw", 16))
    need("v", i_cw)
    k_wm = ts(T.wm[:], T.cw[:], pd, None, A.is_equal)
    k_gf = copy("v", T.gf[:, 0:3], T.gi[:])
    k_gm = ts(T.gm[:], T.cg[:], pd, None, A.is_equal)
    need("v", i_z)
    k_id = [ts(T.id1[:], T.zi[:], 0.0, None, A.is_equal)]
    for l in range(L):
        a = 32 * l + 16
        k = times(T.rl[:, a:a + 16], T.wm[:], T.wf[:, l:l + 1], k_wf, k_wm)
    for l in (1, 2):
        a = 32 * l
        k = times(T.rl[:, a:a + 16], T.gm[:], T.gf[:, l:l + 1], k_gf, k_gm)
    k_id.append(times(T.id64[:], T.id1[:], 64.0, k_id[0]))
    k = lists_mm(16, 96, k, k_list[0])
    need("v", k)
    k_list[1] = k_list[2] = k_wl[0] = k_wl[1] = k_wl[2] = ts(T.lists[:, 16:96], T.pl[:, 16:96], 2.0, pt, A.mult, A.add)

    for l in range(L):
        inputs(l, 0)
        addresses(l, 0)
        lookups(l, 0)
        inputs(l, 1)
        pick(l, 0)
        addresses(l, 1)
        codes(l, 0)
        lookups(l, 1)
        pick(l, 1)
        codes(l, 1)

    for k in "ys":
        need(k, *ds_tok[L, 0], *ds_tok[L, 1])
    for a in range(8):
        q["ys"[a % 2]].dma_start(T.y[16 * a:16 * a + 16, :], T.yt[:, a, :]).then_inc(T.sem.sty, 16)
    for l in range(L):
        for h in range(2):
            need("g", ("sent%d%d" % (l, h), n - 1))
    need("g", ("sty", 128), ("qg", cnt["g"]), ("qv", cnt["v"]), ("qs", cnt["s"]), ("qp", cnt["p"]))
